import numpy as np
import ml_dtypes


def mxq(x, axis, fmt="e4m3"):
    dtype, down = {"e4m3": (ml_dtypes.float8_e4m3fn, 7), "e5m2": (ml_dtypes.float8_e5m2, 14)}[fmt]
    v = np.moveaxis(np.asarray(x, np.float32).astype(ml_dtypes.bfloat16).astype(np.float64), axis, -1)
    blocks = v.reshape(v.shape[:-1] + (-1, 32))
    amax = np.abs(blocks).max(-1, keepdims=True)
    byte = np.maximum(np.where(amax > 0, np.frexp(amax)[1] - 1 + 127, 0) - down, 1)
    scale = np.exp2(byte - 127.0)
    codes = (blocks / scale).astype(np.float32).astype(dtype).astype(np.float64)
    return np.moveaxis((codes * scale).reshape(v.shape), -1, axis)


WIDE = False


def mx_kscale(k):
    if not WIDE:
        return np.ones(k)
    levels = np.array([10, -10, 5, -5, 0])
    if k % 512:
        return np.exp2(np.random.permutation(np.resize(levels, k // 32))).repeat(32)
    a = np.empty((k // 512, 16))
    for p in range(k // 512):
        a[p, :8] = np.random.permutation(np.resize(levels, 8))
        for g in range(8):
            far = levels[np.abs(levels - a[p, g]) >= 10]
            a[p, g + 8] = far[np.random.randint(len(far))]
    return np.exp2(a.ravel()).repeat(32)


def f64(x):
    return np.asarray(x).astype(np.float64)


def striped(idx):
    return np.tile(idx.reshape(-1, 16).T, (8, 1)).astype(np.uint16)


def unstriped(offs):
    return offs[:16].T.reshape(-1).astype(np.int64)


def striped8(idx):
    return np.concatenate([x.reshape(-1, 16).T for x in idx]).astype(np.uint16)


def runs(offs, k):
    lists = np.stack([offs[16 * r : 16 * r + 16].T.reshape(-1) for r in range(8)]).astype(np.int64)
    return lists[np.arange(k) % 512 // 64]


def pack_weight(w):
    k, n = w.shape
    w = f64(np.asarray(w, np.float32).astype(ml_dtypes.bfloat16)).reshape(k // 32, 32, n)
    amax = np.abs(w).max(1)
    byte = np.clip(np.where(amax > 0, np.frexp(amax)[1] - 1 + 127 - 7, 1), 1, 254)
    scaled = (w * np.exp2(127.0 - byte)[:, None, :]).reshape(k, n).astype(np.float32)
    words = np.ascontiguousarray(scaled.reshape(k // 512, 128, 4, n).transpose(0, 1, 3, 2)).astype(ml_dtypes.float8_e4m3fn).view(np.uint8)
    return words, np.ascontiguousarray(byte.astype(np.uint8).reshape(k // 512, 16, n))


def unpack_weight(words, scales):
    g, p, n, _ = words.shape
    vals = np.ascontiguousarray(words).view(ml_dtypes.float8_e4m3fn).astype(np.float64) * np.repeat(np.exp2(scales.astype(np.float64) - 127.0), 8, axis=1)[..., None]
    return vals.transpose(0, 1, 3, 2).reshape(g * 512, n)


K, T, S, G, H, W, C = 512, 1024, 256, 2048, 512, 128, 512


def setup_inputs():
    n = np.random.standard_normal
    s = mx_kscale(K)[:, None]
    packed_xT = pack_weight(n((K, T)) * s)
    packed_dT = pack_weight(n((K, G)) / s)
    perm = np.random.permutation(S)
    return {
        "x_words": packed_xT[0],
        "x_scales": packed_xT[1],
        "d_words": packed_dT[0],
        "d_scales": packed_dT[1],
        "gs": (np.random.uniform(0.5, 1.5, (K, 1)) / s).astype(np.float32),
        "offs": striped8(np.random.randint(0, T, (8, S))),
        "k1": striped8(np.random.randint(0, G, (8, H))),
        "n1": striped(perm[:W]),
        "n2": striped(perm[W:]),
        "n3": striped(np.random.permutation(S)),
        "cand": striped8(np.random.randint(0, T, (8, C))),
        "n4": striped(np.random.permutation(S)),
        "n5": striped(np.random.permutation(S)),
    }


def reference(x_words, x_scales, d_words, d_scales, gs, offs, k1, n1, n2, n3, cand, n4, n5):
    x_cand = unpack_weight(x_words, x_scales)[np.arange(K)[:, None], runs(cand, K)]
    d_k1 = unpack_weight(d_words, d_scales)[np.arange(K)[:, None], runs(k1, K)]
    xq = unpack_weight(x_words, x_scales)[np.arange(K)[:, None], runs(offs, K)]
    h = 0.0625 * (d_k1.T @ xq)
    pa = h[:, unstriped(n1)]
    pb = h[:, unstriped(n2)]
    rb = pa - pb
    ds = np.zeros((H, S))
    ds[:, unstriped(n1)] = pb
    dt = ds.copy()
    dt[:, unstriped(n2)] = rb
    z = f64(gs) * (np.maximum(dt, 0.5 * dt[:, unstriped(n3)]))
    s = 0.0625 * ((x_cand.T @ mxq(z, 0, "e4m3")))
    st = np.maximum(s, s[:, unstriped(n4)])
    ds2 = np.zeros((C, S))
    ds2[:, unstriped(n5)] = st
    return ds2 - s

@@ -1,0 +1,176 @@
+from contextlib import ExitStack
+
+import concourse.mybir as mybir
+
+K, T, S, G, H, W, C = 512, 1024, 256, 2048, 512, 128, 512
+FLOPS = 2 * K * H * S + 2 * K * C * S
+
+F32 = mybir.dt.float32
+BF16 = mybir.dt.bfloat16
+I32 = mybir.dt.int32
+U32 = mybir.dt.uint32
+U16 = mybir.dt.uint16
+U8 = mybir.dt.uint8
+FP8X4 = mybir.dt.float8_e4m3fn_x4
+COPY = mybir.ActivationFunctionType.Copy
+MULT = mybir.AluOpType.mult
+MAX = mybir.AluOpType.max
+SUB = mybir.AluOpType.subtract
+
+P = 128
+PACK = 4
+SEND_WINDOW = 384
+HALVES = ((0, 128), (128, 256))
+PIECES = ((0, 128), (128, 192), (192, 256))
+
+
+def tile_picked_hpqhswapdsendhop_none_p_kernel(tc, x_words, x_scales, d_words, d_scales, gs, offs, k1, n1, n2, n3, cand, n4, n5, out):
+    nc = tc.nc
+    with ExitStack() as ctx:
+        lists = ctx.enter_context(tc.tile_pool(name="lists", bufs=1))
+        keep = ctx.enter_context(tc.tile_pool(name="keep", bufs=1))
+        psum = ctx.enter_context(tc.psum_pool(name="psum", bufs=1))
+
+        def load_list(src, name):
+            tile = lists.tile(list(src.shape), U16, name=name)
+            nc.sync.dma_start(tile[:], src)
+            return tile
+
+        offs_l = load_list(offs, "offs_l")
+        k1_l = load_list(k1, "k1_l")
+        d_bytes = keep.tile([P, G], U8, name="d_bytes")
+        x_bytes = keep.tile([P, T], U8, name="x_bytes")
+        for tile, rows in ((x_bytes, x_scales), (d_bytes, d_scales)):
+            words = rows[0].bitcast(I32)
+            nc.scalar.dma_start(tile[:].bitcast(I32), words.unsqueeze(1).to_broadcast([16, 8, words.shape[1]]))
+        d_table = keep.tile([P, G], U32, name="d_table")
+        x_table = keep.tile([P, T], U32, name="x_table")
+        nc.scalar.dma_start(d_table[:].bitcast(I32), d_words[0].rearrange("p n t -> p (n t)").bitcast(I32))
+        nc.scalar.dma_start(x_table[:].bitcast(I32), x_words[0].rearrange("p n t -> p (n t)").bitcast(I32))
+        n2_l = load_list(n2, "n2_l")
+        n1_l = load_list(n1, "n1_l")
+        n3_l = load_list(n3, "n3_l")
+        cand_l = load_list(cand, "cand_l")
+        n4_l = load_list(n4, "n4_l")
+        n5_l = load_list(n5, "n5_l")
+        gain = keep.tile([P, PACK], F32, name="gain")
+        nc.gpsimd.dma_start(gain[:], gs.rearrange("(p t) o -> p (t o)", t=PACK))
+
+        first_planes = keep.tile([P, H + S], U8, name="first_planes", align_bytes=64)
+        cand_plane = keep.tile([P, C], U8, name="cand_plane", align_bytes=64)
+
+
+        def place_rows(queue, plane, picked):
+            nc.vector.tensor_copy(plane[:].bitcast(I32), picked[:].bitcast(I32))
+            for i in range(1, 4):
+                queue.dma_start(plane[i:P:32, :].bitcast(I32), picked[8 * i : P : 32, :].bitcast(I32))
+
+        first_picked = keep.tile([P, H + S], U8, name="first_picked")
+        nc.vector.tensor_copy(first_picked[:, H:], x_bytes[:].indirect(offs_l[:]))
+        nc.vector.tensor_copy(first_picked[:, :H], d_bytes[:].indirect(k1_l[:]))
+        place_rows(nc.sync, first_planes, first_picked)
+
+        d_picked = keep.tile([P, H], U32, name="d_picked")
+        nc.vector.tensor_copy(d_picked[:], d_table[:].indirect(k1_l[:]))
+        d_dealt = keep.tile([P, H], U32, name="d_dealt", tag="stationary_words", align_bytes=64)
+        nc.vector.tensor_copy(d_dealt[:].rearrange("p (t m) -> p m t", t=PACK), d_picked[:].rearrange("p (m t) -> p m t", t=PACK))
+        xq = keep.tile([P, S], U32, name="xq", align_bytes=64)
+        nc.vector.tensor_copy(xq[:], x_table[:].indirect(offs_l[:]))
+        d_plane = keep.tile([P, H], U8, name="d_plane", tag="stationary_bytes", align_bytes=64)
+
+        h = []
+        for t in range(PACK):
+            cols = slice(t * P, (t + 1) * P)
+            nc.vector.tensor_copy(d_plane[:, cols], first_planes[:, t:H:PACK])
+            acc = psum.tile([P, S], F32, name="h_acc%d" % t, tag="bank%d" % t)
+            nc.tensor.matmul_mx(out=acc[:], lhsT=d_dealt[:, cols].bitcast(FP8X4), lhsT_scale=d_plane[:, cols],
+                                rhs=xq[:].bitcast(FP8X4), rhs_scale=first_planes[:, H:], start=True, stop=True)
+            h_t = keep.tile([P, S], F32, name="h%d" % t)
+            if t == 0:
+                nc.scalar.activation(h_t[:], acc[:], COPY, scale=0.0625)
+            else:
+                nc.vector.tensor_scalar(h_t[:], acc[:], 0.0625, None, MULT)
+            h.append(h_t)
+
+        z = keep.tile([P, S, PACK], BF16, name="z", align_bytes=64)
+        cand_words = keep.tile([P, C], U32, name="cand_words", tag="stationary_words", align_bytes=64)
+        cand_picked = keep.tile([P, C], U8, name="cand_picked", tag="stationary_bytes", align_bytes=64)
+        half = S // 2
+        pb = [keep.tile([P, W], F32, name="pb%d" % t) for t in range(PACK)]
+        rb = [keep.tile([P, W], F32, name="rb%d" % t) for t in range(PACK)]
+        dt = [keep.tile([P, S], F32, name="dt%d" % t) for t in range(PACK)]
+
+        def fetch_pair(t):
+            pa = keep.tile([P, W], F32, name="pa%d" % t)
+            nc.scalar.activation(pb[t][:], h[t][:].indirect(n2_l[:]), COPY)
+            nc.scalar.activation(pa[:], h[t][:].indirect(n1_l[:]), COPY)
+            nc.vector.tensor_tensor(rb[t][:], pa[:], pb[t][:], SUB)
+
+        def hop(t):
+            far = keep.tile([P, S], F32, name="dt_far%d" % t)
+            big = keep.tile([P, S], F32, name="big%d" % t)
+            for lo, hi in PIECES if t == PACK - 1 else HALVES:
+                nc.scalar.activation(far[:, lo:hi], dt[t][:].indirect(n3_l[:, lo // 16 : hi // 16]), COPY)
+                nc.vector.scalar_tensor_tensor(big[:, lo:hi], far[:, lo:hi], 0.5, dt[t][:, lo:hi], MULT, MAX)
+                nc.vector.tensor_scalar(z[:, lo:hi, t], big[:, lo:hi], gain[:, t : t + 1], None, MULT)
+
+        def pick_cand(t):
+            piece = slice((t % 2) * 256, (t % 2 + 1) * 256)
+            piece_l = cand_l[:, (t % 2) * 16 : (t % 2 + 1) * 16]
+            if t < 2:
+                nc.vector.tensor_copy(cand_picked[:, piece], x_bytes[:].indirect(piece_l))
+            else:
+                nc.vector.tensor_copy(cand_words[:, piece], x_table[:].indirect(piece_l))
+
+        fetch_pair(0)
+        nc.scalar.activation(dt[0][:].indirect(n1_l[:]), pb[0][:], COPY)
+        for t in range(PACK):
+            if t + 1 < PACK:
+                fetch_pair(t + 1)
+            pick_cand(t)
+            if t == 1:
+                place_rows(nc.sync, cand_plane, cand_picked)
+            nc.scalar.activation(dt[t][:].indirect(n2_l[:]), rb[t][:], COPY)
+            if t + 1 < PACK:
+                nc.scalar.activation(dt[t + 1][:].indirect(n1_l[:]), pb[t + 1][:], COPY)
+            hop(t)
+
+        z_words = keep.tile([P, S], U32, name="z_words", align_bytes=64)
+        z_plane = keep.tile([P, S], U8, name="z_plane", align_bytes=64)
+        for lo, hi in PIECES:
+            nc.vector.quantize_mx(out=z_words[:, lo:hi].bitcast(FP8X4), scales=z_plane[:, lo:hi], in_=z[:, lo:hi, :].rearrange("p j t -> p (j t)"))
+
+        s = [keep.tile([P, S], F32, name="s%d" % c) for c in range(C // P)]
+        st = [keep.tile([P, S], F32, name="st%d" % c) for c in range(C // P)]
+
+        def score(c):
+            cols = slice(c * P, (c + 1) * P)
+            if c == 0:
+                for b, (lo, hi) in enumerate(PIECES):
+                    acc = psum.tile([P, hi - lo], F32, name="s_piece%d" % b, tag="bank%d" % b)
+                    nc.tensor.matmul_mx(out=acc[:], lhsT=cand_words[:, cols].bitcast(FP8X4), lhsT_scale=cand_plane[:, cols],
+                                        rhs=z_words[:, lo:hi].bitcast(FP8X4), rhs_scale=z_plane[:, lo:hi], start=True, stop=True)
+                    nc.scalar.activation(s[c][:, lo:hi], acc[:], COPY, scale=0.0625)
+            else:
+                acc = psum.tile([P, S], F32, name="s_acc%d" % c)
+                nc.tensor.matmul_mx(out=acc[:], lhsT=cand_words[:, cols].bitcast(FP8X4), lhsT_scale=cand_plane[:, cols],
+                                    rhs=z_words[:].bitcast(FP8X4), rhs_scale=z_plane[:], start=True, stop=True)
+                nc.vector.tensor_scalar(s[c][:], acc[:], 0.0625, None, MULT)
+            far = keep.tile([P, S], F32, name="s_far%d" % c)
+            for u in range(2):
+                part = slice(u * half, (u + 1) * half)
+                nc.scalar.activation(far[:, part], s[c][:].indirect(n4_l[:, u * half // 16 : (u + 1) * half // 16]), COPY)
+                nc.vector.tensor_tensor(st[c][:, part], far[:, part], s[c][:, part], MAX)
+
+        def send(c):
+            ds2 = keep.tile([P, SEND_WINDOW], F32, name="ds2_%d" % c)
+            nc.scalar.activation(ds2[:].indirect(n5_l[:]), st[c][:], COPY)
+            res = keep.tile([P, S], F32, name="res%d" % c)
+            nc.vector.tensor_tensor(res[:], ds2[:, :S], s[c][:], SUB)
+            nc.sync.dma_start(out[c * P : (c + 1) * P, :], res[:])
+
+        score(0)
+        for c in range(C // P):
+            if c + 1 < C // P:
+                score(c + 1)
+            send(c)

@@ -20,7 +20,8 @@ SUB = mybir.AluOpType.subtract
 P = 128
 PACK = 4
 SEND_WINDOW = 384
-HALVES = ((0, 128), (128, 256))
+FETCH_WINDOW = 272
+HALVES = ((0, 256),)
 PIECES = ((0, 128), (128, 192), (192, 256))
 
 
@@ -36,59 +37,69 @@ def tile_picked_hpqhswapdsendhop_none_p_kernel(tc, x_words, x_scales, d_words, d
             nc.sync.dma_start(tile[:], src)
             return tile
 
-        offs_l = load_list(offs, "offs_l")
-        k1_l = load_list(k1, "k1_l")
-        d_bytes = keep.tile([P, G], U8, name="d_bytes")
-        x_bytes = keep.tile([P, T], U8, name="x_bytes")
-        for tile, rows in ((x_bytes, x_scales), (d_bytes, d_scales)):
+        def load_scale_rows(rows, name):
             words = rows[0].bitcast(I32)
-            nc.scalar.dma_start(tile[:].bitcast(I32), words.unsqueeze(1).to_broadcast([16, 8, words.shape[1]]))
-        d_table = keep.tile([P, G], U32, name="d_table")
-        x_table = keep.tile([P, T], U32, name="x_table")
-        nc.scalar.dma_start(d_table[:].bitcast(I32), d_words[0].rearrange("p n t -> p (n t)").bitcast(I32))
-        nc.scalar.dma_start(x_table[:].bitcast(I32), x_words[0].rearrange("p n t -> p (n t)").bitcast(I32))
+            tile = keep.tile([P, rows.shape[2]], U8, name=name)
+            nc.sync.dma_start(tile[:].bitcast(I32), words.unsqueeze(1).to_broadcast([16, 8, words.shape[1]]))
+            return tile
+
+        def load_words(words, name):
+            tile = keep.tile([P, words.shape[2]], U32, name=name)
+            nc.sync.dma_start(tile[:].bitcast(I32), words[0].rearrange("p n t -> p (n t)").bitcast(I32))
+            return tile
+
+        offs_l = load_list(offs, "offs_l")
+        x_bytes = load_scale_rows(x_scales, "x_bytes")
+        k1_l = load_list(k1, "k1_l")
+        d_bytes = load_scale_rows(d_scales, "d_bytes")
         n2_l = load_list(n2, "n2_l")
         n1_l = load_list(n1, "n1_l")
         n3_l = load_list(n3, "n3_l")
+        d_table = load_words(d_words, "d_table")
+        x_table = load_words(x_words, "x_table")
         cand_l = load_list(cand, "cand_l")
         n4_l = load_list(n4, "n4_l")
         n5_l = load_list(n5, "n5_l")
         gain = keep.tile([P, PACK], F32, name="gain")
         nc.gpsimd.dma_start(gain[:], gs.rearrange("(p t) o -> p (t o)", t=PACK))
 
-        first_planes = keep.tile([P, H + S], U8, name="first_planes", align_bytes=64)
+        first_planes = keep.tile([P, H + S], U8, name="first_planes", tag="stationary_bytes", align_bytes=64)
         cand_plane = keep.tile([P, C], U8, name="cand_plane", align_bytes=64)
 
 
-        def place_rows(queue, plane, picked):
-            nc.vector.tensor_copy(plane[:].bitcast(I32), picked[:].bitcast(I32))
+        def place_rows(plane):
             for i in range(1, 4):
-                queue.dma_start(plane[i:P:32, :].bitcast(I32), picked[8 * i : P : 32, :].bitcast(I32))
+                nc.sync.dma_start(plane[i:P:32, :].bitcast(I32), plane[8 * i : P : 32, :].bitcast(I32))
 
         first_picked = keep.tile([P, H + S], U8, name="first_picked")
         nc.vector.tensor_copy(first_picked[:, H:], x_bytes[:].indirect(offs_l[:]))
+        nc.vector.tensor_copy(first_planes[:, H:].bitcast(I32), first_picked[:, H:].bitcast(I32))
         nc.vector.tensor_copy(first_picked[:, :H], d_bytes[:].indirect(k1_l[:]))
-        place_rows(nc.sync, first_planes, first_picked)
+        nc.vector.tensor_copy(first_planes[:, :H].rearrange("p (t m) -> p m t", t=PACK), first_picked[:, :H].rearrange("p (m t) -> p m t", t=PACK))
+        place_rows(first_planes)
 
         d_picked = keep.tile([P, H], U32, name="d_picked")
         nc.vector.tensor_copy(d_picked[:], d_table[:].indirect(k1_l[:]))
         d_dealt = keep.tile([P, H], U32, name="d_dealt", tag="stationary_words", align_bytes=64)
         nc.vector.tensor_copy(d_dealt[:].rearrange("p (t m) -> p m t", t=PACK), d_picked[:].rearrange("p (m t) -> p m t", t=PACK))
         xq = keep.tile([P, S], U32, name="xq", align_bytes=64)
-        nc.vector.tensor_copy(xq[:], x_table[:].indirect(offs_l[:]))
-        d_plane = keep.tile([P, H], U8, name="d_plane", tag="stationary_bytes", align_bytes=64)
+        for lo, hi in ((0, 128), (128, 256)):
+            nc.vector.tensor_copy(xq[:, lo:hi], x_table[:].indirect(offs_l[:, lo // 16 : hi // 16]))
 
         h = []
         for t in range(PACK):
             cols = slice(t * P, (t + 1) * P)
-            nc.vector.tensor_copy(d_plane[:, cols], first_planes[:, t:H:PACK])
-            acc = psum.tile([P, S], F32, name="h_acc%d" % t, tag="bank%d" % t)
-            nc.tensor.matmul_mx(out=acc[:], lhsT=d_dealt[:, cols].bitcast(FP8X4), lhsT_scale=d_plane[:, cols],
-                                rhs=xq[:].bitcast(FP8X4), rhs_scale=first_planes[:, H:], start=True, stop=True)
             h_t = keep.tile([P, S], F32, name="h%d" % t)
             if t == 0:
-                nc.scalar.activation(h_t[:], acc[:], COPY, scale=0.0625)
+                for b, (lo, hi) in enumerate(((0, 128), (128, 256))):
+                    acc = psum.tile([P, hi - lo], F32, name="h_piece%d" % b, tag="bank%d" % (4 * b))
+                    nc.tensor.matmul_mx(out=acc[:], lhsT=d_dealt[:, cols].bitcast(FP8X4), lhsT_scale=first_planes[:, cols],
+                                        rhs=xq[:, lo:hi].bitcast(FP8X4), rhs_scale=first_planes[:, H + lo : H + hi], start=True, stop=True)
+                    nc.scalar.activation(h_t[:, lo:hi], acc[:], COPY, scale=0.0625)
             else:
+                acc = psum.tile([P, S], F32, name="h_acc%d" % t, tag="bank%d" % t)
+                nc.tensor.matmul_mx(out=acc[:], lhsT=d_dealt[:, cols].bitcast(FP8X4), lhsT_scale=first_planes[:, cols],
+                                    rhs=xq[:].bitcast(FP8X4), rhs_scale=first_planes[:, H:], start=True, stop=True)
                 nc.vector.tensor_scalar(h_t[:], acc[:], 0.0625, None, MULT)
             h.append(h_t)
 
@@ -98,7 +109,7 @@ def tile_picked_hpqhswapdsendhop_none_p_kernel(tc, x_words, x_scales, d_words, d
         half = S // 2
         pb = [keep.tile([P, W], F32, name="pb%d" % t) for t in range(PACK)]
         rb = [keep.tile([P, W], F32, name="rb%d" % t) for t in range(PACK)]
-        dt = [keep.tile([P, S], F32, name="dt%d" % t) for t in range(PACK)]
+        dt = [keep.tile([P, FETCH_WINDOW], F32, name="dt%d" % t) for t in range(PACK)]
 
         def fetch_pair(t):
             pa = keep.tile([P, W], F32, name="pa%d" % t)
@@ -129,7 +140,8 @@ def tile_picked_hpqhswapdsendhop_none_p_kernel(tc, x_words, x_scales, d_words, d
                 fetch_pair(t + 1)
             pick_cand(t)
             if t == 1:
-                place_rows(nc.sync, cand_plane, cand_picked)
+                nc.vector.tensor_copy(cand_plane[:].bitcast(I32), cand_picked[:].bitcast(I32))
+                place_rows(cand_plane)
             nc.scalar.activation(dt[t][:].indirect(n2_l[:]), rb[t][:], COPY)
             if t + 1 < PACK:
                 nc.scalar.activation(dt[t + 1][:].indirect(n1_l[:]), pb[t + 1][:], COPY)
@@ -140,7 +152,7 @@ def tile_picked_hpqhswapdsendhop_none_p_kernel(tc, x_words, x_scales, d_words, d
         for lo, hi in PIECES:
             nc.vector.quantize_mx(out=z_words[:, lo:hi].bitcast(FP8X4), scales=z_plane[:, lo:hi], in_=z[:, lo:hi, :].rearrange("p j t -> p (j t)"))
 
-        s = [keep.tile([P, S], F32, name="s%d" % c) for c in range(C // P)]
+        s = [keep.tile([P, FETCH_WINDOW], F32, name="s%d" % c) for c in range(C // P)]
         st = [keep.tile([P, S], F32, name="st%d" % c) for c in range(C // P)]
 
         def score(c):
@@ -155,22 +167,21 @@ def tile_picked_hpqhswapdsendhop_none_p_kernel(tc, x_words, x_scales, d_words, d
                 acc = psum.tile([P, S], F32, name="s_acc%d" % c)
                 nc.tensor.matmul_mx(out=acc[:], lhsT=cand_words[:, cols].bitcast(FP8X4), lhsT_scale=cand_plane[:, cols],
                                     rhs=z_words[:].bitcast(FP8X4), rhs_scale=z_plane[:], start=True, stop=True)
-                nc.vector.tensor_scalar(s[c][:], acc[:], 0.0625, None, MULT)
+                nc.vector.tensor_scalar(s[c][:, :S], acc[:], 0.0625, None, MULT)
             far = keep.tile([P, S], F32, name="s_far%d" % c)
-            for u in range(2):
-                part = slice(u * half, (u + 1) * half)
-                nc.scalar.activation(far[:, part], s[c][:].indirect(n4_l[:, u * half // 16 : (u + 1) * half // 16]), COPY)
-                nc.vector.tensor_tensor(st[c][:, part], far[:, part], s[c][:, part], MAX)
+            nc.scalar.activation(far[:], s[c][:].indirect(n4_l[:]), COPY)
+            nc.vector.tensor_tensor(st[c][:], far[:], s[c][:, :S], MAX)
 
         def send(c):
             ds2 = keep.tile([P, SEND_WINDOW], F32, name="ds2_%d" % c)
             nc.scalar.activation(ds2[:].indirect(n5_l[:]), st[c][:], COPY)
             res = keep.tile([P, S], F32, name="res%d" % c)
-            nc.vector.tensor_tensor(res[:], ds2[:, :S], s[c][:], SUB)
+            nc.vector.tensor_tensor(res[:], ds2[:, :S], s[c][:, :S], SUB)
             nc.sync.dma_start(out[c * P : (c + 1) * P, :], res[:])
 
         score(0)
+        score(1)
         for c in range(C // P):
-            if c + 1 < C // P:
-                score(c + 1)
+            if c + 2 < C // P:
+                score(c + 2)
             send(c)

@@ -37,10 +37,11 @@ def tile_picked_hpqhswapdsendhop_none_p_kernel(tc, x_words, x_scales, d_words, d
             nc.sync.dma_start(tile[:], src)
             return tile
 
-        def load_scale_rows(rows, name):
+        def load_scale_rows(rows, name, clearer):
             words = rows[0].bitcast(I32)
-            tile = keep.tile([P, rows.shape[2]], U8, name=name)
-            nc.sync.dma_start(tile[:].bitcast(I32), words.unsqueeze(1).to_broadcast([16, 8, words.shape[1]]))
+            tile = keep.tile([P, rows.shape[2]], U8, name=name, align_bytes=64)
+            clearer.memset(tile[:].bitcast(I32), 0)
+            nc.scalar.dma_start(tile[0:P:8, :].bitcast(I32), words)
             return tile
 
         def load_words(words, name):
@@ -49,9 +50,9 @@ def tile_picked_hpqhswapdsendhop_none_p_kernel(tc, x_words, x_scales, d_words, d
             return tile
 
         offs_l = load_list(offs, "offs_l")
-        x_bytes = load_scale_rows(x_scales, "x_bytes")
+        x_bytes = load_scale_rows(x_scales, "x_bytes", nc.gpsimd)
         k1_l = load_list(k1, "k1_l")
-        d_bytes = load_scale_rows(d_scales, "d_bytes")
+        d_bytes = load_scale_rows(d_scales, "d_bytes", nc.vector)
         n2_l = load_list(n2, "n2_l")
         n1_l = load_list(n1, "n1_l")
         n3_l = load_list(n3, "n3_l")
@@ -78,11 +79,11 @@ def tile_picked_hpqhswapdsendhop_none_p_kernel(tc, x_words, x_scales, d_words, d
         nc.vector.tensor_copy(first_planes[:, :H].rearrange("p (t m) -> p m t", t=PACK), first_picked[:, :H].rearrange("p (m t) -> p m t", t=PACK))
         place_rows(first_planes)
 
-        d_picked = keep.tile([P, H], U32, name="d_picked")
+        d_picked = keep.tile([P, H], U32, name="d_picked", tag="first_picked")
         nc.vector.tensor_copy(d_picked[:], d_table[:].indirect(k1_l[:]))
         d_dealt = keep.tile([P, H], U32, name="d_dealt", tag="stationary_words", align_bytes=64)
         nc.vector.tensor_copy(d_dealt[:].rearrange("p (t m) -> p m t", t=PACK), d_picked[:].rearrange("p (m t) -> p m t", t=PACK))
-        xq = keep.tile([P, S], U32, name="xq", align_bytes=64)
+        xq = keep.tile([P, S], U32, name="xq", tag="d_bytes", align_bytes=64)
         for lo, hi in ((0, 128), (128, 256)):
             nc.vector.tensor_copy(xq[:, lo:hi], x_table[:].indirect(offs_l[:, lo // 16 : hi // 16]))
 

from contextlib import ExitStack

import concourse.mybir as mybir

K, T, S, G, H, W, C = 512, 1024, 256, 2048, 512, 128, 512
FLOPS = 2 * K * H * S + 2 * K * C * S

F32 = mybir.dt.float32
BF16 = mybir.dt.bfloat16
I32 = mybir.dt.int32
U32 = mybir.dt.uint32
U16 = mybir.dt.uint16
U8 = mybir.dt.uint8
FP8X4 = mybir.dt.float8_e4m3fn_x4
COPY = mybir.ActivationFunctionType.Copy
MULT = mybir.AluOpType.mult
MAX = mybir.AluOpType.max
SUB = mybir.AluOpType.subtract

P = 128
PACK = 4
SEND_WINDOW = 384
FETCH_WINDOW = 272
HALVES = ((0, 256),)
PIECES = ((0, 128), (128, 192), (192, 256))


def tile_picked_hpqhswapdsendhop_none_p_kernel(tc, x_words, x_scales, d_words, d_scales, gs, offs, k1, n1, n2, n3, cand, n4, n5, out):
    nc = tc.nc
    with ExitStack() as ctx:
        lists = ctx.enter_context(tc.tile_pool(name="lists", bufs=1))
        keep = ctx.enter_context(tc.tile_pool(name="keep", bufs=1))
        psum = ctx.enter_context(tc.psum_pool(name="psum", bufs=1))

        def load_list(src, name):
            tile = lists.tile(list(src.shape), U16, name=name)
            nc.sync.dma_start(tile[:], src)
            return tile

        def load_scale_rows(rows, name, clearer):
            words = rows[0].bitcast(I32)
            tile = keep.tile([P, rows.shape[2]], U8, name=name, align_bytes=64)
            clearer.memset(tile[:].bitcast(I32), 0)
            nc.scalar.dma_start(tile[0:P:8, :].bitcast(I32), words)
            return tile

        def load_words(words, name):
            tile = keep.tile([P, words.shape[2]], U32, name=name)
            nc.sync.dma_start(tile[:].bitcast(I32), words[0].rearrange("p n t -> p (n t)").bitcast(I32))
            return tile

        offs_l = load_list(offs, "offs_l")
        x_bytes = load_scale_rows(x_scales, "x_bytes", nc.gpsimd)
        k1_l = load_list(k1, "k1_l")
        d_bytes = load_scale_rows(d_scales, "d_bytes", nc.vector)
        n2_l = load_list(n2, "n2_l")
        n1_l = load_list(n1, "n1_l")
        n3_l = load_list(n3, "n3_l")
        d_table = load_words(d_words, "d_table")
        x_table = load_words(x_words, "x_table")
        cand_l = load_list(cand, "cand_l")
        n4_l = load_list(n4, "n4_l")
        n5_l = load_list(n5, "n5_l")
        gain = keep.tile([P, PACK], F32, name="gain")
        nc.gpsimd.dma_start(gain[:], gs.rearrange("(p t) o -> p (t o)", t=PACK))

        first_planes = keep.tile([P, H + S], U8, name="first_planes", tag="stationary_bytes", align_bytes=64)
        cand_plane = keep.tile([P, C], U8, name="cand_plane", align_bytes=64)


        def place_rows(plane):
            for i in range(1, 4):
                nc.sync.dma_start(plane[i:P:32, :].bitcast(I32), plane[8 * i : P : 32, :].bitcast(I32))

        first_picked = keep.tile([P, H + S], U8, name="first_picked")
        nc.vector.tensor_copy(first_picked[:, H:], x_bytes[:].indirect(offs_l[:]))
        nc.vector.tensor_copy(first_planes[:, H:].bitcast(I32), first_picked[:, H:].bitcast(I32))
        nc.vector.tensor_copy(first_picked[:, :H], d_bytes[:].indirect(k1_l[:]))
        nc.vector.tensor_copy(first_planes[:, :H].rearrange("p (t m) -> p m t", t=PACK), first_picked[:, :H].rearrange("p (m t) -> p m t", t=PACK))
        place_rows(first_planes)

        d_picked = keep.tile([P, H], U32, name="d_picked", tag="first_picked")
        nc.vector.tensor_copy(d_picked[:], d_table[:].indirect(k1_l[:]))
        d_dealt = keep.tile([P, H], U32, name="d_dealt", tag="stationary_words", align_bytes=64)
        nc.vector.tensor_copy(d_dealt[:].rearrange("p (t m) -> p m t", t=PACK), d_picked[:].rearrange("p (m t) -> p m t", t=PACK))
        xq = keep.tile([P, S], U32, name="xq", tag="d_bytes", align_bytes=64)
        for lo, hi in ((0, 128), (128, 256)):
            nc.vector.tensor_copy(xq[:, lo:hi], x_table[:].indirect(offs_l[:, lo // 16 : hi // 16]))

        h = []
        for t in range(PACK):
            cols = slice(t * P, (t + 1) * P)
            h_t = keep.tile([P, S], F32, name="h%d" % t)
            if t == 0:
                for b, (lo, hi) in enumerate(((0, 128), (128, 256))):
                    acc = psum.tile([P, hi - lo], F32, name="h_piece%d" % b, tag="bank%d" % (4 * b))
                    nc.tensor.matmul_mx(out=acc[:], lhsT=d_dealt[:, cols].bitcast(FP8X4), lhsT_scale=first_planes[:, cols],
                                        rhs=xq[:, lo:hi].bitcast(FP8X4), rhs_scale=first_planes[:, H + lo : H + hi], start=True, stop=True)
                    nc.scalar.activation(h_t[:, lo:hi], acc[:], COPY, scale=0.0625)
            else:
                acc = psum.tile([P, S], F32, name="h_acc%d" % t, tag="bank%d" % t)
                nc.tensor.matmul_mx(out=acc[:], lhsT=d_dealt[:, cols].bitcast(FP8X4), lhsT_scale=first_planes[:, cols],
                                    rhs=xq[:].bitcast(FP8X4), rhs_scale=first_planes[:, H:], start=True, stop=True)
                nc.vector.tensor_scalar(h_t[:], acc[:], 0.0625, None, MULT)
            h.append(h_t)

        z = keep.tile([P, S, PACK], BF16, name="z", align_bytes=64)
        cand_words = keep.tile([P, C], U32, name="cand_words", tag="stationary_words", align_bytes=64)
        cand_picked = keep.tile([P, C], U8, name="cand_picked", tag="stationary_bytes", align_bytes=64)
        half = S // 2
        pb = [keep.tile([P, W], F32, name="pb%d" % t) for t in range(PACK)]
        rb = [keep.tile([P, W], F32, name="rb%d" % t) for t in range(PACK)]
        dt = [keep.tile([P, FETCH_WINDOW], F32, name="dt%d" % t) for t in range(PACK)]

        def fetch_pair(t):
            pa = keep.tile([P, W], F32, name="pa%d" % t)
            nc.scalar.activation(pb[t][:], h[t][:].indirect(n2_l[:]), COPY)
            nc.scalar.activation(pa[:], h[t][:].indirect(n1_l[:]), COPY)
            nc.vector.tensor_tensor(rb[t][:], pa[:], pb[t][:], SUB)

        def hop(t):
            far = keep.tile([P, S], F32, name="dt_far%d" % t)
            big = keep.tile([P, S], F32, name="big%d" % t)
            for lo, hi in PIECES if t == PACK - 1 else HALVES:
                nc.scalar.activation(far[:, lo:hi], dt[t][:].indirect(n3_l[:, lo // 16 : hi // 16]), COPY)
                nc.vector.scalar_tensor_tensor(big[:, lo:hi], far[:, lo:hi], 0.5, dt[t][:, lo:hi], MULT, MAX)
                nc.vector.tensor_scalar(z[:, lo:hi, t], big[:, lo:hi], gain[:, t : t + 1], None, MULT)

        def pick_cand(t):
            piece = slice((t % 2) * 256, (t % 2 + 1) * 256)
            piece_l = cand_l[:, (t % 2) * 16 : (t % 2 + 1) * 16]
            if t < 2:
                nc.vector.tensor_copy(cand_picked[:, piece], x_bytes[:].indirect(piece_l))
            else:
                nc.vector.tensor_copy(cand_words[:, piece], x_table[:].indirect(piece_l))

        fetch_pair(0)
        nc.scalar.activation(dt[0][:].indirect(n1_l[:]), pb[0][:], COPY)
        for t in range(PACK):
            if t + 1 < PACK:
                fetch_pair(t + 1)
            pick_cand(t)
            if t == 1:
                nc.vector.tensor_copy(cand_plane[:].bitcast(I32), cand_picked[:].bitcast(I32))
                place_rows(cand_plane)
            nc.scalar.activation(dt[t][:].indirect(n2_l[:]), rb[t][:], COPY)
            if t + 1 < PACK:
                nc.scalar.activation(dt[t + 1][:].indirect(n1_l[:]), pb[t + 1][:], COPY)
            hop(t)

        z_words = keep.tile([P, S], U32, name="z_words", align_bytes=64)
        z_plane = keep.tile([P, S], U8, name="z_plane", align_bytes=64)
        for lo, hi in PIECES:
            nc.vector.quantize_mx(out=z_words[:, lo:hi].bitcast(FP8X4), scales=z_plane[:, lo:hi], in_=z[:, lo:hi, :].rearrange("p j t -> p (j t)"))

        s = [keep.tile([P, FETCH_WINDOW], F32, name="s%d" % c) for c in range(C // P)]
        st = [keep.tile([P, S], F32, name="st%d" % c) for c in range(C // P)]

        def score(c):
            cols = slice(c * P, (c + 1) * P)
            if c == 0:
                for b, (lo, hi) in enumerate(PIECES):
                    acc = psum.tile([P, hi - lo], F32, name="s_piece%d" % b, tag="bank%d" % b)
                    nc.tensor.matmul_mx(out=acc[:], lhsT=cand_words[:, cols].bitcast(FP8X4), lhsT_scale=cand_plane[:, cols],
                                        rhs=z_words[:, lo:hi].bitcast(FP8X4), rhs_scale=z_plane[:, lo:hi], start=True, stop=True)
                    nc.scalar.activation(s[c][:, lo:hi], acc[:], COPY, scale=0.0625)
            else:
                acc = psum.tile([P, S], F32, name="s_acc%d" % c)
                nc.tensor.matmul_mx(out=acc[:], lhsT=cand_words[:, cols].bitcast(FP8X4), lhsT_scale=cand_plane[:, cols],
                                    rhs=z_words[:].bitcast(FP8X4), rhs_scale=z_plane[:], start=True, stop=True)
                nc.vector.tensor_scalar(s[c][:, :S], acc[:], 0.0625, None, MULT)
            far = keep.tile([P, S], F32, name="s_far%d" % c)
            nc.scalar.activation(far[:], s[c][:].indirect(n4_l[:]), COPY)
            nc.vector.tensor_tensor(st[c][:], far[:], s[c][:, :S], MAX)

        def send(c):
            ds2 = keep.tile([P, SEND_WINDOW], F32, name="ds2_%d" % c)
            nc.scalar.activation(ds2[:].indirect(n5_l[:]), st[c][:], COPY)
            res = keep.tile([P, S], F32, name="res%d" % c)
            nc.vector.tensor_tensor(res[:], ds2[:, :S], s[c][:, :S], SUB)
            nc.sync.dma_start(out[c * P : (c + 1) * P, :], res[:])

        score(0)
        score(1)
        for c in range(C // P):
            if c + 2 < C // P:
                score(c + 2)
            send(c)
